import numpy as np, ml_dtypes
CORES = [9,13,81,85,89,93,97,101,113,117,121,125]
N = 12
C = 128
def setup_inputs(rng):
    u = np.triu(np.ones((128, 128), np.float32)).astype(ml_dtypes.bfloat16)
    return {"x": rng.standard_normal((N, 128, C), dtype=np.float32).astype(ml_dtypes.bfloat16), "u": np.broadcast_to(u, (N, 128, 128)).copy()}
def setup_inputs_big(rng):
    d = setup_inputs(rng)
    for k in ("x",): d[k] = (d[k].astype(np.float32) * 1048576.0).astype(d[k].dtype)
    return d
def setup_inputs_small(rng):
    d = setup_inputs(rng)
    for k in ("x",): d[k] = (d[k].astype(np.float32) * (1 / 1048576.0)).astype(d[k].dtype)
    return d
def setup_inputs_apart(rng):
    d = setup_inputs(rng)
    f = (10.0 ** rng.permutation(np.linspace(-1.5, 1.5, N))).astype(np.float32).reshape(N, 1, 1)
    for k in ("x",): d[k] = (d[k].astype(np.float32) * f).astype(d[k].dtype)
    return d
def reference(x, u):
    X, U = x.astype(np.float64), u.astype(np.float64)
    y = np.zeros((N, 128, C)); c = np.zeros(C)
    for r in range(N):
        y[r] = U[r].T @ X[r] + c
        c = c + X[r].sum(axis=0)
    return {"y": y.astype(ml_dtypes.bfloat16 if x.dtype != np.float64 else np.float64)}

@@ -1,0 +1,113 @@
+from concourse.bass import DstId, RemoteDMATransfer
+
+N_RANKS = 12
+SCRATCH = {
+    "xs": ("sbuf", [128, 128], "bfloat16"),
+    "us": ("sbuf", [128, 128], "bfloat16"),
+    "ones": ("sbuf", [128, 128], "bfloat16"),
+    "tcol": ("sbuf", [128, 8], "bfloat16"),
+    "q": ("sbuf", [128, 128], "bfloat16"),
+    "ys": ("sbuf", [128, 128], "bfloat16"),
+    "relay": ("dram", [128, 1], "bfloat16"),
+    "sums": ("dram", [N_RANKS, 128, 1], "bfloat16"),
+    "pt": ("psum", [128, 512], "float32"),
+    "py": ("psum", [128, 512], "float32"),
+}
+SEMAPHORES = ["xl", "ul", "ql", "st", "fill", "mm1", "cp1", "mm2", "cp2", "arrived", "sent"]
+
+HOP1_ENGINES = 8
+HOP2_PER_ENGINE = 6
+
+
+def _engines(mask, first, count):
+    bits = [1 << b for b in range(mask.bit_length()) if (mask >> b) & 1]
+    return sum(bits[first:first + count])
+
+
+def _relays(cores, topo):
+    group, used, relay = set(cores), set(), {}
+    for s, c in enumerate(cores[:-1]):
+        later = cores[s + 1:]
+        if len(later) == 1 and topo.may_write(c, later[0]):
+            relay[s] = None
+            continue
+        cand = [h for h in range(topo.CHIPS * topo.CORES_PER_CHIP)
+                if topo.chip(h) == topo.chip(c) and h not in group and h not in used
+                and all(topo.may_write(h, d) for d in later)]
+        cand.sort(key=lambda h: (topo.die(h) != topo.die(c), h))
+        relay[s] = cand[0]
+        used.add(cand[0])
+    return relay
+
+
+def _relay_program(g, core, s, cores, T, topo):
+    later = cores[s + 1:]
+    common = topo.mask(core, later[0])
+    for d in later:
+        common &= topo.mask(core, d)
+    k = -(-len(later) // HOP2_PER_ENGINE)
+    transfers = []
+    for j in range(k):
+        part = later[j::k]
+        ids = []
+        for d in part:
+            rid, pid, _se = topo.addr(d)
+            ids.append(DstId(rid=rid, pnc=pid))
+        transfers.append(RemoteDMATransfer(dst_ids=ids, dma_engine_mask=_engines(common, j, 1),
+                                           remote_sem=T.sem.arrived, srcs=[T.relay[:]],
+                                           dsts=[T.sums[s] for _d in part], alu_op=0))
+    g.wait_ge(T.sem.arrived, HOP1_ENGINES)
+    g.remote_dma_fused(transfers, local_sem=T.sem.sent)
+    g.wait_ge(T.sem.sent, k)
+
+
+def rank_program(g, core, T, topo):
+    cores = list(T.cores)
+    relay = _relays(cores, topo)
+    rank = T.rank_of(core)
+    if rank is None:
+        for s in relay:
+            if relay[s] == core:
+                _relay_program(g, core, s, cores, T, topo)
+        return
+    sem = T.sem
+    sends = rank < len(cores) - 1
+
+    g.sync.dma_start(T.xs[:], T.x[:]).then_inc(sem.xl, 16)
+    g.vector.memset(T.ones[:], 1.0).then_inc(sem.fill, 1)
+    if sends:
+        g.scalar.wait_ge(sem.sent, HOP1_ENGINES)
+    else:
+        g.scalar.wait_ge(sem.xl, 16)
+    g.scalar.dma_start(T.us[:], T.u[:]).then_inc(sem.ul, 16)
+
+    g.tensor.wait_ge(sem.xl, 16)
+    g.tensor.wait_ge(sem.fill, 1)
+    if sends:
+        g.tensor.matmul(T.pt[:, 0:1], T.xs[:], T.ones[:, 0:1], True, True).then_inc(sem.mm1, 1)
+        g.vector.wait_ge(sem.mm1, 1)
+        g.vector.tensor_copy(T.tcol[:, 0:1], T.pt[:, 0:1]).then_inc(sem.cp1, 1)
+        to = relay[rank]
+        out = T.relay[:]
+        if to is None:
+            to = cores[rank + 1]
+            out = T.sums[rank]
+        rid, pid, _se = topo.addr(to)
+        g.wait_ge(sem.cp1, 1)
+        g.remote_dma(out, T.tcol[:, 0:1], sem.arrived, sem.sent, pid, rid,
+                     _engines(topo.mask(core, to), 0, HOP1_ENGINES))
+
+    g.tensor.wait_ge(sem.ul, 16)
+    mm = g.tensor.matmul(T.py[:, 0:128], T.us[:], T.xs[:], True, rank == 0)
+    if rank > 0:
+        due = sum(1 if relay[s] is not None else HOP1_ENGINES for s in range(rank))
+        g.sync.wait_ge(sem.arrived, due)
+        g.sync.dma_start(T.q[0:rank, :], T.sums[0:rank]).then_inc(sem.ql, 16)
+        g.tensor.wait_ge(sem.ql, 16)
+        mm = g.tensor.matmul(T.py[:, 0:128], T.ones[0:rank, :], T.q[0:rank, :], False, True)
+    mm.then_inc(sem.mm2, 1)
+    g.vector.wait_ge(sem.mm2, 1)
+    g.vector.tensor_copy(T.ys[:], T.py[:, 0:128]).then_inc(sem.cp2, 1)
+    g.sync.wait_ge(sem.cp2, 1)
+    g.sync.dma_start(T.y[:], T.ys[:]).then_inc(sem.st, 16)
+    g.sync.wait_ge(sem.st, 16)

@@ -1,4 +1,5 @@
 from concourse.bass import DstId, RemoteDMATransfer
+from concourse.mybir import AluOpType
 
 N_RANKS = 12
 SCRATCH = {
@@ -13,10 +14,10 @@ SCRATCH = {
     "pt": ("psum", [128, 512], "float32"),
     "py": ("psum", [128, 512], "float32"),
 }
-SEMAPHORES = ["xl", "ul", "ql", "st", "fill", "mm1", "cp1", "mm2", "cp2", "arrived", "sent"]
+SEMAPHORES = ["xl", "ul", "ql", "st", "fill", "tri", "mm1", "cp1", "mm2", "cp2", "arrived", "sent"]
 
 HOP1_ENGINES = 8
-HOP2_PER_ENGINE = 6
+RELAY_ENGINES = 8
 
 
 def _engines(mask, first, count):
@@ -41,11 +42,20 @@ def _relays(cores, topo):
 
 
 def _relay_program(g, core, s, cores, T, topo):
+    sem = T.sem
     later = cores[s + 1:]
-    common = topo.mask(core, later[0])
+    common = topo.mask(core, cores[s])
     for d in later:
         common &= topo.mask(core, d)
-    k = -(-len(later) // HOP2_PER_ENGINE)
+
+    g.vector.memset(T.ones[:], 1.0).then_inc(sem.fill, 1)
+    g.wait_ge(sem.fill, 1)
+    g.affine_select(T.us[:], T.ones[:], [[1, 128]], AluOpType.is_ge, 0.0, 0, -1).then_inc(sem.tri, 1)
+    g.wait_ge(sem.tri, 1)
+    rid, pid, _se = topo.addr(cores[s])
+    g.remote_dma(T.us[:], T.us[:], sem.ul, sem.sent, pid, rid, _engines(common, 0, RELAY_ENGINES))
+
+    k = min(RELAY_ENGINES, len(later))
     transfers = []
     for j in range(k):
         part = later[j::k]
@@ -54,11 +64,11 @@ def _relay_program(g, core, s, cores, T, topo):
             rid, pid, _se = topo.addr(d)
             ids.append(DstId(rid=rid, pnc=pid))
         transfers.append(RemoteDMATransfer(dst_ids=ids, dma_engine_mask=_engines(common, j, 1),
-                                           remote_sem=T.sem.arrived, srcs=[T.relay[:]],
+                                           remote_sem=sem.arrived, srcs=[T.relay[:]],
                                            dsts=[T.sums[s] for _d in part], alu_op=0))
-    g.wait_ge(T.sem.arrived, HOP1_ENGINES)
-    g.remote_dma_fused(transfers, local_sem=T.sem.sent)
-    g.wait_ge(T.sem.sent, k)
+    g.wait_ge(sem.arrived, HOP1_ENGINES)
+    g.remote_dma_fused(transfers, local_sem=sem.sent)
+    g.wait_ge(sem.sent, RELAY_ENGINES + k)
 
 
 def rank_program(g, core, T, topo):
@@ -72,14 +82,18 @@ def rank_program(g, core, T, topo):
         return
     sem = T.sem
     sends = rank < len(cores) - 1
+    has_relay = sends and relay[rank] is not None
 
     g.sync.dma_start(T.xs[:], T.x[:]).then_inc(sem.xl, 16)
     g.vector.memset(T.ones[:], 1.0).then_inc(sem.fill, 1)
-    if sends:
-        g.scalar.wait_ge(sem.sent, HOP1_ENGINES)
-    else:
-        g.scalar.wait_ge(sem.xl, 16)
-    g.scalar.dma_start(T.us[:], T.u[:]).then_inc(sem.ul, 16)
+    u_due = RELAY_ENGINES
+    if not has_relay:
+        u_due = 16
+        if sends:
+            g.scalar.wait_ge(sem.sent, HOP1_ENGINES)
+        else:
+            g.scalar.wait_ge(sem.xl, 16)
+        g.scalar.dma_start(T.us[:], T.u[:]).then_inc(sem.ul, 16)
 
     g.tensor.wait_ge(sem.xl, 16)
     g.tensor.wait_ge(sem.fill, 1)
@@ -96,8 +110,10 @@ def rank_program(g, core, T, topo):
         g.wait_ge(sem.cp1, 1)
         g.remote_dma(out, T.tcol[:, 0:1], sem.arrived, sem.sent, pid, rid,
                      _engines(topo.mask(core, to), 0, HOP1_ENGINES))
+        if has_relay:
+            g.wait_ge(sem.sent, HOP1_ENGINES)
 
-    g.tensor.wait_ge(sem.ul, 16)
+    g.tensor.wait_ge(sem.ul, u_due)
     mm = g.tensor.matmul(T.py[:, 0:128], T.us[:], T.xs[:], True, rank == 0)
     if rank > 0:
         due = sum(1 if relay[s] is not None else HOP1_ENGINES for s in range(rank))

@@ -2,9 +2,11 @@ from concourse.bass import DstId, RemoteDMATransfer
 from concourse.mybir import AluOpType
 
 N_RANKS = 12
+HALF = 64
 SCRATCH = {
     "xs": ("sbuf", [128, 128], "bfloat16"),
     "us": ("sbuf", [128, 128], "bfloat16"),
+    "uh": ("sbuf", [128, HALF], "bfloat16"),
     "ones": ("sbuf", [128, 128], "bfloat16"),
     "tcol": ("sbuf", [128, 8], "bfloat16"),
     "q": ("sbuf", [128, 128], "bfloat16"),
@@ -41,19 +43,35 @@ def _relays(cores, topo):
     return relay
 
 
-def _relay_program(g, core, s, cores, T, topo):
+def _partner(s, cores, relay, topo):
+    if relay.get(s) is None:
+        return None
+    for p, c in enumerate(cores):
+        if p != s and topo.chip(c) == topo.chip(cores[s]) and relay.get(p) is not None:
+            return p
+    return None
+
+
+def _send_half(g, T, topo, first, to, mask):
+    sem = T.sem
+    g.wait_ge(sem.fill, 1)
+    g.affine_select(T.uh[:], T.ones[:, 0:HALF], [[1, HALF]], AluOpType.is_ge, 0.0, first, -1).then_inc(sem.tri, 1)
+    g.wait_ge(sem.tri, 1)
+    rid, pid, _se = topo.addr(to)
+    g.remote_dma(T.us[:, first:first + HALF], T.uh[:], sem.ul, sem.sent, pid, rid, mask)
+
+
+def _relay_program(g, core, s, built, cores, T, topo):
     sem = T.sem
     later = cores[s + 1:]
     common = topo.mask(core, cores[s])
     for d in later:
         common &= topo.mask(core, d)
-
-    g.vector.memset(T.ones[:], 1.0).then_inc(sem.fill, 1)
-    g.wait_ge(sem.fill, 1)
-    g.affine_select(T.us[:], T.ones[:], [[1, 128]], AluOpType.is_ge, 0.0, 0, -1).then_inc(sem.tri, 1)
-    g.wait_ge(sem.tri, 1)
-    rid, pid, _se = topo.addr(cores[s])
-    g.remote_dma(T.us[:], T.us[:], sem.ul, sem.sent, pid, rid, _engines(common, 0, RELAY_ENGINES))
+    left = 0
+    if built:
+        g.vector.memset(T.ones[:], 1.0).then_inc(sem.fill, 1)
+        _send_half(g, T, topo, 0, cores[s], _engines(common, 0, RELAY_ENGINES))
+        left = RELAY_ENGINES
 
     k = min(RELAY_ENGINES, len(later))
     transfers = []
@@ -68,7 +86,7 @@ def _relay_program(g, core, s, cores, T, topo):
                                            dsts=[T.sums[s] for _d in part], alu_op=0))
     g.wait_ge(sem.arrived, HOP1_ENGINES)
     g.remote_dma_fused(transfers, local_sem=sem.sent)
-    g.wait_ge(sem.sent, RELAY_ENGINES + k)
+    g.wait_ge(sem.sent, left + k)
 
 
 def rank_program(g, core, T, topo):
@@ -78,16 +96,21 @@ def rank_program(g, core, T, topo):
     if rank is None:
         for s in relay:
             if relay[s] == core:
-                _relay_program(g, core, s, cores, T, topo)
+                _relay_program(g, core, s, _partner(s, cores, relay, topo) is not None, cores, T, topo)
         return
     sem = T.sem
     sends = rank < len(cores) - 1
-    has_relay = sends and relay[rank] is not None
+    partner = _partner(rank, cores, relay, topo)
 
     g.sync.dma_start(T.xs[:], T.x[:]).then_inc(sem.xl, 16)
     g.vector.memset(T.ones[:], 1.0).then_inc(sem.fill, 1)
-    u_due = RELAY_ENGINES
-    if not has_relay:
+    left = 0
+    if partner is not None:
+        u_due = RELAY_ENGINES + HOP1_ENGINES
+        to = cores[partner]
+        _send_half(g, T, topo, HALF, to, _engines(topo.mask(core, to), 0, HOP1_ENGINES))
+        left = HOP1_ENGINES
+    else:
         u_due = 16
         if sends:
             g.scalar.wait_ge(sem.sent, HOP1_ENGINES)
@@ -110,8 +133,8 @@ def rank_program(g, core, T, topo):
         g.wait_ge(sem.cp1, 1)
         g.remote_dma(out, T.tcol[:, 0:1], sem.arrived, sem.sent, pid, rid,
                      _engines(topo.mask(core, to), 0, HOP1_ENGINES))
-        if has_relay:
-            g.wait_ge(sem.sent, HOP1_ENGINES)
+        if partner is not None:
+            g.wait_ge(sem.sent, left + HOP1_ENGINES)
 
     g.tensor.wait_ge(sem.ul, u_due)
     mm = g.tensor.matmul(T.py[:, 0:128], T.us[:], T.xs[:], True, rank == 0)

from concourse.bass import DstId, RemoteDMATransfer
from concourse.mybir import AluOpType

N_RANKS = 12
HALF = 64
SCRATCH = {
    "xs": ("sbuf", [128, 128], "bfloat16"),
    "us": ("sbuf", [128, 128], "bfloat16"),
    "uh": ("sbuf", [128, HALF], "bfloat16"),
    "ones": ("sbuf", [128, 128], "bfloat16"),
    "tcol": ("sbuf", [128, 8], "bfloat16"),
    "q": ("sbuf", [128, 128], "bfloat16"),
    "ys": ("sbuf", [128, 128], "bfloat16"),
    "relay": ("dram", [128, 1], "bfloat16"),
    "sums": ("dram", [N_RANKS, 128, 1], "bfloat16"),
    "pt": ("psum", [128, 512], "float32"),
    "py": ("psum", [128, 512], "float32"),
}
SEMAPHORES = ["xl", "ul", "ql", "st", "fill", "tri", "mm1", "cp1", "mm2", "cp2", "arrived", "sent"]

HOP1_ENGINES = 8
RELAY_ENGINES = 8


def _engines(mask, first, count):
    bits = [1 << b for b in range(mask.bit_length()) if (mask >> b) & 1]
    return sum(bits[first:first + count])


def _relays(cores, topo):
    group, used, relay = set(cores), set(), {}
    for s, c in enumerate(cores[:-1]):
        later = cores[s + 1:]
        if len(later) == 1 and topo.may_write(c, later[0]):
            relay[s] = None
            continue
        cand = [h for h in range(topo.CHIPS * topo.CORES_PER_CHIP)
                if topo.chip(h) == topo.chip(c) and h not in group and h not in used
                and all(topo.may_write(h, d) for d in later)]
        cand.sort(key=lambda h: (topo.die(h) != topo.die(c), h))
        relay[s] = cand[0]
        used.add(cand[0])
    return relay


def _partner(s, cores, relay, topo):
    if relay.get(s) is None:
        return None
    for p, c in enumerate(cores):
        if p != s and topo.chip(c) == topo.chip(cores[s]) and relay.get(p) is not None:
            return p
    return None


def _send_half(g, T, topo, first, to, mask):
    sem = T.sem
    g.wait_ge(sem.fill, 1)
    g.affine_select(T.uh[:], T.ones[:, 0:HALF], [[1, HALF]], AluOpType.is_ge, 0.0, first, -1).then_inc(sem.tri, 1)
    g.wait_ge(sem.tri, 1)
    rid, pid, _se = topo.addr(to)
    g.remote_dma(T.us[:, first:first + HALF], T.uh[:], sem.ul, sem.sent, pid, rid, mask)


def _relay_program(g, core, s, built, cores, T, topo):
    sem = T.sem
    later = cores[s + 1:]
    common = topo.mask(core, cores[s])
    for d in later:
        common &= topo.mask(core, d)
    left = 0
    if built:
        g.vector.memset(T.ones[:], 1.0).then_inc(sem.fill, 1)
        _send_half(g, T, topo, 0, cores[s], _engines(common, 0, RELAY_ENGINES))
        left = RELAY_ENGINES

    k = min(RELAY_ENGINES, len(later))
    transfers = []
    for j in range(k):
        part = later[j::k]
        ids = []
        for d in part:
            rid, pid, _se = topo.addr(d)
            ids.append(DstId(rid=rid, pnc=pid))
        transfers.append(RemoteDMATransfer(dst_ids=ids, dma_engine_mask=_engines(common, j, 1),
                                           remote_sem=sem.arrived, srcs=[T.relay[:]],
                                           dsts=[T.sums[s] for _d in part], alu_op=0))
    g.wait_ge(sem.arrived, HOP1_ENGINES)
    g.remote_dma_fused(transfers, local_sem=sem.sent)
    g.wait_ge(sem.sent, left + k)


def rank_program(g, core, T, topo):
    cores = list(T.cores)
    relay = _relays(cores, topo)
    rank = T.rank_of(core)
    if rank is None:
        for s in relay:
            if relay[s] == core:
                _relay_program(g, core, s, _partner(s, cores, relay, topo) is not None, cores, T, topo)
        return
    sem = T.sem
    sends = rank < len(cores) - 1
    partner = _partner(rank, cores, relay, topo)

    g.sync.dma_start(T.xs[:], T.x[:]).then_inc(sem.xl, 16)
    g.vector.memset(T.ones[:], 1.0).then_inc(sem.fill, 1)
    left = 0
    if partner is not None:
        u_due = RELAY_ENGINES + HOP1_ENGINES
        to = cores[partner]
        _send_half(g, T, topo, HALF, to, _engines(topo.mask(core, to), 0, HOP1_ENGINES))
        left = HOP1_ENGINES
    else:
        u_due = 16
        if sends:
            g.scalar.wait_ge(sem.sent, HOP1_ENGINES)
        else:
            g.scalar.wait_ge(sem.xl, 16)
        g.scalar.dma_start(T.us[:], T.u[:]).then_inc(sem.ul, 16)

    g.tensor.wait_ge(sem.xl, 16)
    g.tensor.wait_ge(sem.fill, 1)
    if sends:
        g.tensor.matmul(T.pt[:, 0:1], T.xs[:], T.ones[:, 0:1], True, True).then_inc(sem.mm1, 1)
        g.vector.wait_ge(sem.mm1, 1)
        g.vector.tensor_copy(T.tcol[:, 0:1], T.pt[:, 0:1]).then_inc(sem.cp1, 1)
        to = relay[rank]
        out = T.relay[:]
        if to is None:
            to = cores[rank + 1]
            out = T.sums[rank]
        rid, pid, _se = topo.addr(to)
        g.wait_ge(sem.cp1, 1)
        g.remote_dma(out, T.tcol[:, 0:1], sem.arrived, sem.sent, pid, rid,
                     _engines(topo.mask(core, to), 0, HOP1_ENGINES))
        if partner is not None:
            g.wait_ge(sem.sent, left + HOP1_ENGINES)

    g.tensor.wait_ge(sem.ul, u_due)
    mm = g.tensor.matmul(T.py[:, 0:128], T.us[:], T.xs[:], True, rank == 0)
    if rank > 0:
        due = sum(1 if relay[s] is not None else HOP1_ENGINES for s in range(rank))
        g.sync.wait_ge(sem.arrived, due)
        g.sync.dma_start(T.q[0:rank, :], T.sums[0:rank]).then_inc(sem.ql, 16)
        g.tensor.wait_ge(sem.ql, 16)
        mm = g.tensor.matmul(T.py[:, 0:128], T.ones[0:rank, :], T.q[0:rank, :], False, True)
    mm.then_inc(sem.mm2, 1)
    g.vector.wait_ge(sem.mm2, 1)
    g.vector.tensor_copy(T.ys[:], T.py[:, 0:128]).then_inc(sem.cp2, 1)
    g.sync.wait_ge(sem.cp2, 1)
    g.sync.dma_start(T.y[:], T.ys[:]).then_inc(sem.st, 16)
    g.sync.wait_ge(sem.st, 16)
